import numpy as np
import ml_dtypes


def mxq(x, axis, fmt="e4m3"):
    dtype, down = {"e4m3": (ml_dtypes.float8_e4m3fn, 7), "e5m2": (ml_dtypes.float8_e5m2, 14)}[fmt]
    v = np.moveaxis(np.asarray(x, np.float32).astype(ml_dtypes.bfloat16).astype(np.float64), axis, -1)
    blocks = v.reshape(v.shape[:-1] + (-1, 32))
    amax = np.abs(blocks).max(-1, keepdims=True)
    byte = np.maximum(np.where(amax > 0, np.frexp(amax)[1] - 1 + 127, 0) - down, 1)
    scale = np.exp2(byte - 127.0)
    codes = (blocks / scale).astype(np.float32).astype(dtype).astype(np.float64)
    return np.moveaxis((codes * scale).reshape(v.shape), -1, axis)


WIDE = False


def mx_kscale(k):
    if not WIDE:
        return np.ones(k)
    levels = np.array([30, -30])
    if k % 512:
        return np.exp2(np.random.permutation(np.resize(levels, k // 32))).repeat(32)
    a = np.empty((k // 512, 16))
    for p in range(k // 512):
        a[p, :8] = np.random.permutation(np.resize(levels, 8))
        for g in range(8):
            far = levels[np.abs(levels - a[p, g]) >= 10]
            a[p, g + 8] = far[np.random.randint(len(far))]
    return np.exp2(a.ravel()).repeat(32)


def f64(x):
    return np.asarray(x).astype(np.float64)


def striped(idx):
    return np.tile(np.asarray(idx).reshape(-1, 16).T, (8, 1)).astype(np.uint16)


def unstriped(offs):
    return offs[:16].T.reshape(-1).astype(np.int64)


E2M1 = np.array([0.0, 0.5, 1.0, 1.5, 2.0, 3.0, 4.0, 6.0, -0.0, -0.5, -1.0, -1.5, -2.0, -3.0, -4.0, -6.0])


def pack_weight(w, fmt):
    k, n = w.shape
    w = f64(np.asarray(w, np.float32).astype(ml_dtypes.bfloat16)).reshape(k // 32, 32, n)
    amax = np.abs(w).max(1)
    if fmt == "e4m3":
        byte = np.frexp(amax)[1] - 1 + 127 - 7
    else:
        mant, ex = np.frexp(amax / 6.0)
        byte = np.where(mant > 0.5, ex, ex - 1) + 127
    byte = np.clip(np.where(amax > 0, byte, 1), 1, 254)
    scaled = (w * np.exp2(127.0 - byte)[:, None, :]).reshape(k, n).astype(np.float32)
    by_word = np.ascontiguousarray(scaled.reshape(k // 512, 128, 4, n).transpose(0, 1, 3, 2))
    if fmt == "e4m3":
        words = by_word.astype(ml_dtypes.float8_e4m3fn).view(np.uint8)
    else:
        c = by_word.astype(ml_dtypes.float4_e2m1fn).view(np.uint8) & 0xF
        words = (c[..., 0::2] | (c[..., 1::2] << 4)).reshape(k // 512, 128, 2 * n)
    return np.ascontiguousarray(words), np.ascontiguousarray(byte.astype(np.uint8).reshape(k // 512, 16, n))


def unpack_weight(words, scales, fmt):
    g, _, n = scales.shape
    words = np.ascontiguousarray(words).reshape(g, 128, n, -1)
    if fmt == "e4m3":
        vals = words.view(ml_dtypes.float8_e4m3fn).astype(np.float64)
    else:
        nib = np.empty((g, 128, n, 4), np.uint8)
        nib[..., 0::2] = words & 0xF
        nib[..., 1::2] = words >> 4
        vals = E2M1[nib]
    vals = vals * np.repeat(np.exp2(scales.astype(np.float64) - 127.0), 8, axis=1)[..., None]
    return vals.transpose(0, 1, 3, 2).reshape(g * 512, n)


K, J, N, R, T, V, Q = 512, 512, 256, 256, 1024, 1024, 1024


def setup_inputs():
    n = np.random.standard_normal
    idx = np.random.permutation(T)[:J]
    idx2 = np.random.permutation(V)[:J]
    idx3 = np.random.permutation(Q)[:N]
    fj = mx_kscale(J)
    fk = mx_kscale(K)
    drp = pack_weight(n((K, R)) * 1 / np.sqrt(K) / fk[:, None], "e2m1")
    return {
        "xf": (n((K, T))).astype(np.float32),
        "ra": (np.random.uniform(0.5, 1.5, (1, J)) * fj).astype(np.float32),
        "lo": (np.random.uniform(-0.3, 0.5, (K, 1))).astype(np.float32),
        "gt": (n((N, V)) * np.exp(0.5 * n((1, V)))).astype(np.float32),
        "rb": (np.random.uniform(0.5, 1.5, (1, J)) / fj).astype(np.float32),
        "pr": (n((N, J))).astype(np.float32),
        "fkr": (np.random.uniform(0.5, 1.5, (1, K)) * fk).astype(np.float32),
        "dr_words": drp[0],
        "dr_scales": drp[1],
        "old": (0.5 * n((R, Q))).astype(np.float32),
        "offs": striped(idx),
        "offs2": striped(idx2),
        "offs3": striped(idx3),
    }


def reference(xf, ra, lo, gt, rb, pr, fkr, dr_words, dr_scales, old, offs, offs2, offs3):
    idx = unstriped(offs)
    idx2 = unstriped(offs2)
    idx3 = unstriped(offs3)
    dru = unpack_weight(dr_words, dr_scales, "e2m1")
    us = np.maximum(f64(xf)[:, idx] - f64(lo), 0.0) * f64(ra)
    ut = us.T
    uj = ut * f64(fkr)
    gs = (f64(gt)[:, idx2] - f64(pr)) * f64(rb)
    gj = gs.T
    ujq = mxq(uj, 0, "e4m3")
    gjq = mxq(gj, 0, "e5m2")
    w = ujq.T @ gjq
    wq = mxq(w, 0, "e5m2")
    v2 = dru.T @ wq
    wp = np.zeros((R, Q))
    wp[:, idx3] = v2
    y = 0.05 * wp + f64(old)
    return y

@@ -1,0 +1,241 @@
+from contextlib import ExitStack
+
+import concourse.mybir as mybir
+from concourse.masks import make_identity
+
+K, J, N, R, T, V, Q = 512, 512, 256, 256, 1024, 1024, 1024
+FLOPS = 2 * J * K * N + 2 * K * R * N
+
+F32 = mybir.dt.float32
+BF16 = mybir.dt.bfloat16
+I32 = mybir.dt.int32
+U32 = mybir.dt.uint32
+U16 = mybir.dt.uint16
+U8 = mybir.dt.uint8
+E4M3 = mybir.dt.float8_e4m3fn_x4
+E5M2 = mybir.dt.float8_e5m2_x4
+E2M1 = mybir.dt.float4_e2m1fn_x4
+ALU = mybir.AluOpType
+COPY = mybir.ActivationFunctionType.Copy
+
+P = 128
+PACK = 4
+
+
+def by_lines_in(ap):
+    return ap.rearrange("p (b i s) -> p b s i", i=PACK, s=PACK)
+
+
+def by_lines_out(ap):
+    return ap.rearrange("p s (b i) -> p b s i", i=PACK)
+
+
+def tile_list_directions_over_errors_placed_kernel(
+    tc, xf, ra, lo, gt, rb, pr, fkr, dr_words, dr_scales, old, offs, offs2, offs3, out
+):
+    nc = tc.nc
+    with ExitStack() as ctx:
+        sb = ctx.enter_context(tc.tile_pool(name="sb", bufs=1))
+        turn = ctx.enter_context(tc.psum_pool(name="turn", bufs=6))
+        sums = ctx.enter_context(tc.psum_pool(name="sums", bufs=1))
+
+        list_x = sb.tile([P, J // 16], U16, name="list_x")
+        list_g = sb.tile([P, J // 16], U16, name="list_g")
+        list_out = sb.tile([P, N // 16], U16, name="list_out")
+        fk4 = sb.tile([P, PACK], F32, name="fk4")
+        ra4 = sb.tile([P, PACK], F32, name="ra4")
+        rb4 = sb.tile([P, PACK], F32, name="rb4")
+        lo4 = sb.tile([P, PACK], F32, name="lo4")
+        gt_sb = [sb.tile([P, V], F32, name=f"gt{h}") for h in range(2)]
+        pr_sb = [sb.tile([P, J], F32, name=f"pr{h}") for h in range(2)]
+        xf_sb = [sb.tile([P, T], F32, name=f"xf{t}") for t in range(PACK)]
+        old_sb = [sb.tile([P, Q], F32, name=f"old{r}") for r in range(2)]
+        page = [sb.tile([P, Q], F32, name=f"page{r}") for r in range(2)]
+        dr_w = sb.tile([P, 2 * R], U8, name="dr_w", align_bytes=64)
+        dr_s = sb.tile([P, R], U8, name="dr_s", align_bytes=64)
+        ident = sb.tile([P, P], F32, name="ident")
+
+        make_identity(nc, ident[:])
+        nc.vector.memset(dr_s[:].bitcast(I32), 0)
+        for r in range(2):
+            nc.vector.memset(page[r][:], 0.0)
+
+        nc.sync.dma_start(out=lo4[:], in_=lo.rearrange("(p t) o -> p (t o)", t=PACK))
+        nc.sync.dma_start(out=fk4[:], in_=fkr.rearrange("o (p t) -> (o p) t", t=PACK))
+        nc.sync.dma_start(out=ra4[:], in_=ra.rearrange("o (p s) -> (o p) s", s=PACK))
+        nc.sync.dma_start(list_x[:], offs)
+        xf_rows = xf.rearrange("(p t) c -> t p c", t=PACK)
+        for t in range(2):
+            nc.sync.dma_start(out=xf_sb[t][:], in_=xf_rows[t])
+        nc.sync.dma_start(out=pr_sb[0][:], in_=pr[:P, :])
+        for t in range(2, PACK):
+            nc.sync.dma_start(out=xf_sb[t][:], in_=xf_rows[t])
+        nc.sync.dma_start(list_g[:], offs2)
+        nc.sync.dma_start(out=rb4[:], in_=rb.rearrange("o (p s) -> (o p) s", s=PACK))
+        nc.sync.dma_start(out=pr_sb[1][:], in_=pr[P:, :])
+        for h in range(2):
+            nc.sync.dma_start(out=gt_sb[h][:], in_=gt[h * P : (h + 1) * P, :])
+        nc.sync.dma_start(out=dr_w[:].bitcast(I32), in_=dr_words[0].bitcast(I32))
+        for quad in range(4):
+            nc.sync.dma_start(
+                out=dr_s[32 * quad : 32 * quad + 4, :].bitcast(I32),
+                in_=dr_scales[0, 4 * quad : 4 * quad + 4, :].bitcast(I32),
+            )
+        nc.sync.dma_start(list_out[:], offs3)
+        for r in range(2):
+            nc.sync.dma_start(out=old_sb[r][:], in_=old[r * P : (r + 1) * P, :])
+
+        neg_lo = sb.tile([P, PACK], F32, name="neg_lo")
+        nc.scalar.activation(neg_lo[:], lo4[:], COPY, scale=-1.0)
+
+        fk_rows = turn.tile([P, PACK, P], F32, name="turned")
+        for t in range(PACK):
+            nc.tensor.transpose(fk_rows[:, t, :], fk4[:, t : t + 1].to_broadcast([P, P]), ident[:])
+        weight = [sb.tile([P, P, PACK], F32, name=f"weight{t}", tag=f"weight{t}", align_bytes=64) for t in range(PACK)]
+        for t in range(PACK):
+            nc.vector.tensor_tensor(
+                weight[t][:],
+                fk_rows[:, t, :].unsqueeze(2).to_broadcast([P, P, PACK]),
+                ra4[:].unsqueeze(1).to_broadcast([P, P, PACK]),
+                ALU.mult,
+            )
+
+        def turn_slots(src):
+            turned = turn.tile([P, PACK, P], F32, name="turned")
+            for s in range(PACK):
+                nc.tensor.transpose(turned[:, s, :], src[:, s, :], ident[:])
+            return turned
+
+        u_turned, u_bf, u_codes, u_scales, x_picked = {}, {}, {}, {}, {}
+
+        def x_gather(t):
+            x_picked[t] = sb.tile([P, J], F32, name=f"x_picked{t}", tag=f"x_picked{t}")
+            nc.scalar.activation(x_picked[t][:], xf_sb[t][:].indirect(list_x[:]), COPY)
+
+        def x_threshold(t, tag):
+            excess = sb.tile([P, PACK, P], F32, name="excess", tag=tag, align_bytes=64)
+            nc.vector.tensor_scalar(
+                by_lines_out(excess[:]), by_lines_in(x_picked[t][:]), neg_lo[:, t : t + 1], 0.0, ALU.add, ALU.max
+            )
+            u_turned[t] = turn_slots(excess)
+
+        def x_weigh(t):
+            u_bf[t] = sb.tile([P, P, PACK], BF16, name=f"u_bf{t}", tag=f"u_bf{t}", align_bytes=64)
+            nc.vector.tensor_tensor(u_bf[t][:], u_turned[t][:].rearrange("p s m -> p m s"), weight[t][:], ALU.mult)
+
+        def x_quantize(t):
+            u_codes[t] = sb.tile([P, P], U32, name=f"u_codes{t}", align_bytes=64)
+            u_scales[t] = sb.tile([P, P], U8, name=f"u_scales{t}", align_bytes=64)
+            nc.vector.quantize_mx(u_codes[t][:].bitcast(E4M3), u_scales[t][:], u_bf[t][:].rearrange("p m s -> p (m s)"))
+
+        g_turned, g_bf, g_codes, g_scales = {}, {}, {}, {}
+
+        def g_predictions(h, tag):
+            negated = sb.tile([P, PACK, P], F32, name="negated", tag=tag, align_bytes=64)
+            nc.vector.tensor_scalar(by_lines_out(negated[:]), by_lines_in(pr_sb[h][:]), -1.0, None, ALU.mult)
+            g_turned[h] = turn.tile([P, PACK, P], F32, name="turned")
+            for s in range(PACK):
+                nc.tensor.matmul(
+                    g_turned[h][:, s, :], negated[:, s, :], ident[:], start=(s == 0), stop=False, is_transpose=True
+                )
+
+        def g_gather(h, on_vector, tag):
+            picked = sb.tile([P, J], F32, name="picked", tag=tag)
+            cut = J - on_vector
+            nc.scalar.activation(picked[:, :cut], gt_sb[h][:].indirect(list_g[:, : cut // 16]), COPY)
+            if on_vector:
+                nc.vector.tensor_copy(picked[:, cut:], gt_sb[h][:].indirect(list_g[:, cut // 16 :]))
+            for s in range(PACK):
+                nc.tensor.matmul(
+                    g_turned[h][:, s, :], picked[:, s::PACK], ident[:], start=False, stop=(s == PACK - 1), is_transpose=True
+                )
+
+        def g_weigh(h):
+            g_bf[h] = sb.tile([P, P, PACK], BF16, name=f"g_bf{h}", align_bytes=64)
+            nc.vector.tensor_tensor(
+                g_bf[h][:], g_turned[h][:].rearrange("p s n -> p n s"), rb4[:].unsqueeze(1).to_broadcast([P, P, PACK]), ALU.mult
+            )
+
+        w_sum, w_bf, w_codes, w_scales = {}, {}, {}, {}
+
+        def first_product(h):
+            g_codes[h] = sb.tile([P, P], U32, name=f"g_codes{h}", align_bytes=64)
+            g_scales[h] = sb.tile([P, P], U8, name=f"g_scales{h}", align_bytes=64)
+            nc.vector.quantize_mx(g_codes[h][:].bitcast(E5M2), g_scales[h][:], g_bf[h][:].rearrange("p n s -> p (n s)"))
+            w_sum[h] = sums.tile([P, PACK, P], F32, name=f"w_sum{h}")
+            for t in range(PACK):
+                nc.tensor.matmul_mx(
+                    out=w_sum[h][:, t, :],
+                    lhsT=u_codes[t][:].bitcast(E4M3),
+                    lhsT_scale=u_scales[t][:],
+                    rhs=g_codes[h][:].bitcast(E5M2),
+                    rhs_scale=g_scales[h][:],
+                    start=True,
+                    stop=True,
+                )
+            w_bf[h] = sb.tile([P, P, PACK], BF16, name=f"w_bf{h}", align_bytes=64)
+            nc.scalar.copy(w_bf[h][:], w_sum[h][:].rearrange("p t n -> p n t"))
+
+        v_sum = {}
+
+        def second_product(h):
+            w_codes[h] = sb.tile([P, P], U32, name=f"w_codes{h}", align_bytes=64)
+            w_scales[h] = sb.tile([P, P], U8, name=f"w_scales{h}", align_bytes=64)
+            nc.vector.quantize_mx(w_codes[h][:].bitcast(E5M2), w_scales[h][:], w_bf[h][:].rearrange("p n t -> p (n t)"))
+            for r in range(2):
+                v_sum[r, h] = turn.tile([P, P], F32, name="turned")
+                nc.tensor.matmul_mx(
+                    out=v_sum[r, h][:],
+                    lhsT=dr_w[:, 2 * P * r : 2 * P * (r + 1)].bitcast(E2M1),
+                    lhsT_scale=dr_s[:, P * r : P * (r + 1)],
+                    rhs=w_codes[h][:].bitcast(E5M2),
+                    rhs_scale=w_scales[h][:],
+                    start=True,
+                    stop=True,
+                )
+
+        def place(h):
+            places = list_out[:, h * P // 16 : (h + 1) * P // 16]
+            v_sb = [sb.tile([P, P], F32, name=f"v_sb{r}{h}") for r in range(2)]
+            nc.vector.tensor_copy(v_sb[0][:], v_sum[0, h][:])
+            nc.scalar.copy(v_sb[1][:], v_sum[1, h][:])
+            nc.vector.tensor_copy(page[0][:].indirect(places), v_sb[0][:])
+            nc.scalar.activation(page[1][:].indirect(places), v_sb[1][:], COPY)
+
+        x_gather(0)
+        x_gather(1)
+        x_threshold(0, "excess0")
+        g_predictions(0, "negated0")
+        x_gather(2)
+        x_threshold(1, "excess1")
+        x_weigh(0)
+        x_gather(3)
+        x_threshold(2, "weight0")
+        x_weigh(1)
+        x_quantize(0)
+        g_predictions(1, "weight1")
+        x_quantize(1)
+        g_gather(0, 0, "g0")
+        x_threshold(3, "u_bf0")
+        x_weigh(2)
+        g_gather(1, 256, "x_picked3")
+        x_quantize(2)
+        x_weigh(3)
+        x_quantize(3)
+        g_weigh(0)
+        g_weigh(1)
+        first_product(0)
+        first_product(1)
+        second_product(0)
+        second_product(1)
+        place(0)
+        place(1)
+        for r in range(2):
+            for c in range(2):
+                cols = slice(c * Q // 2, (c + 1) * Q // 2)
+                result = sb.tile([P, Q // 2], F32, name=f"result{r}{c}")
+                nc.vector.scalar_tensor_tensor(
+                    result[:], page[r][:, cols], 0.05, old_sb[r][:, cols], ALU.mult, ALU.add
+                )
+                queue = nc.sync if c == 0 else nc.scalar
+                queue.dma_start(out=out[r * P : (r + 1) * P, cols], in_=result[:])

@@ -43,11 +43,11 @@ def tile_list_directions_over_errors_placed_kernel(
         list_g = sb.tile([P, J // 16], U16, name="list_g")
         list_out = sb.tile([P, N // 16], U16, name="list_out")
         fk4 = sb.tile([P, PACK], F32, name="fk4")
-        ra4 = sb.tile([P, PACK], F32, name="ra4")
+        ra4 = sb.tile([P, PACK], F32, name="ra4", tag="ra", align_bytes=64)
         rb4 = sb.tile([P, PACK], F32, name="rb4")
         lo4 = sb.tile([P, PACK], F32, name="lo4")
         gt_sb = [sb.tile([P, V], F32, name=f"gt{h}") for h in range(2)]
-        pr_sb = [sb.tile([P, J], F32, name=f"pr{h}") for h in range(2)]
+        pr_sb = [sb.tile([P, J], F32, name=f"pr{h}", tag=f"pr{h}", align_bytes=64) for h in range(2)]
         xf_sb = [sb.tile([P, T], F32, name=f"xf{t}") for t in range(PACK)]
         old_sb = [sb.tile([P, Q], F32, name=f"old{r}") for r in range(2)]
         page = [sb.tile([P, Q], F32, name=f"page{r}") for r in range(2)]
@@ -109,7 +109,7 @@ def tile_list_directions_over_errors_placed_kernel(
         u_turned, u_bf, u_codes, u_scales, x_picked = {}, {}, {}, {}, {}
 
         def x_gather(t):
-            x_picked[t] = sb.tile([P, J], F32, name=f"x_picked{t}", tag=f"x_picked{t}")
+            x_picked[t] = sb.tile([P, J], F32, name=f"x_picked{t}", tag=f"x_picked{t}", align_bytes=64)
             nc.scalar.activation(x_picked[t][:], xf_sb[t][:].indirect(list_x[:]), COPY)
 
         def x_threshold(t, tag):
@@ -132,7 +132,10 @@ def tile_list_directions_over_errors_placed_kernel(
 
         def g_predictions(h, tag):
             negated = sb.tile([P, PACK, P], F32, name="negated", tag=tag, align_bytes=64)
-            nc.vector.tensor_scalar(by_lines_out(negated[:]), by_lines_in(pr_sb[h][:]), -1.0, None, ALU.mult)
+            if h == 0:
+                nc.vector.tensor_scalar(by_lines_out(negated[:]), by_lines_in(pr_sb[h][:]), -1.0, None, ALU.mult)
+            else:
+                nc.scalar.activation(by_lines_out(negated[:]), by_lines_in(pr_sb[h][:]), COPY, scale=-1.0)
             g_turned[h] = turn.tile([P, PACK, P], F32, name="turned")
             for s in range(PACK):
                 nc.tensor.matmul(
@@ -140,7 +143,7 @@ def tile_list_directions_over_errors_placed_kernel(
                 )
 
         def g_gather(h, on_vector, tag):
-            picked = sb.tile([P, J], F32, name="picked", tag=tag)
+            picked = sb.tile([P, J], F32, name="picked", tag=tag, align_bytes=64)
             cut = J - on_vector
             nc.scalar.activation(picked[:, :cut], gt_sb[h][:].indirect(list_g[:, : cut // 16]), COPY)
             if on_vector:
@@ -204,21 +207,21 @@ def tile_list_directions_over_errors_placed_kernel(
 
         x_gather(0)
         x_gather(1)
-        x_threshold(0, "excess0")
-        g_predictions(0, "negated0")
+        x_threshold(0, "ra")
+        g_predictions(0, "x_picked0")
         x_gather(2)
-        x_threshold(1, "excess1")
+        x_threshold(1, "pr0")
         x_weigh(0)
         x_gather(3)
         x_threshold(2, "weight0")
         x_weigh(1)
         x_quantize(0)
-        g_predictions(1, "weight1")
+        g_predictions(1, "x_picked2")
         x_quantize(1)
-        g_gather(0, 0, "g0")
         x_threshold(3, "u_bf0")
+        g_gather(0, 0, "weight1")
         x_weigh(2)
-        g_gather(1, 256, "x_picked3")
+        g_gather(1, 352, "x_picked3")
         x_quantize(2)
         x_weigh(3)
         x_quantize(3)

@@ -20,6 +20,7 @@ COPY = mybir.ActivationFunctionType.Copy
 
 P = 128
 PACK = 4
+ON_VECTOR = 352
 
 
 def by_lines_in(ap):
@@ -60,18 +61,18 @@ def tile_list_directions_over_errors_placed_kernel(
         for r in range(2):
             nc.vector.memset(page[r][:], 0.0)
 
-        nc.sync.dma_start(out=lo4[:], in_=lo.rearrange("(p t) o -> p (t o)", t=PACK))
         nc.sync.dma_start(out=fk4[:], in_=fkr.rearrange("o (p t) -> (o p) t", t=PACK))
         nc.sync.dma_start(out=ra4[:], in_=ra.rearrange("o (p s) -> (o p) s", s=PACK))
-        nc.sync.dma_start(list_x[:], offs)
+        nc.scalar.dma_start(out=lo4[:], in_=lo.rearrange("(p t) o -> p (t o)", t=PACK))
+        nc.scalar.dma_start(out=rb4[:], in_=rb.rearrange("o (p s) -> (o p) s", s=PACK))
         xf_rows = xf.rearrange("(p t) c -> t p c", t=PACK)
-        for t in range(2):
-            nc.sync.dma_start(out=xf_sb[t][:], in_=xf_rows[t])
+        nc.sync.dma_start(out=xf_sb[0][:], in_=xf_rows[0])
+        nc.sync.dma_start(list_x[:], offs)
+        nc.sync.dma_start(out=xf_sb[1][:], in_=xf_rows[1])
         nc.sync.dma_start(out=pr_sb[0][:], in_=pr[:P, :])
         for t in range(2, PACK):
             nc.sync.dma_start(out=xf_sb[t][:], in_=xf_rows[t])
         nc.sync.dma_start(list_g[:], offs2)
-        nc.sync.dma_start(out=rb4[:], in_=rb.rearrange("o (p s) -> (o p) s", s=PACK))
         nc.sync.dma_start(out=pr_sb[1][:], in_=pr[P:, :])
         for h in range(2):
             nc.sync.dma_start(out=gt_sb[h][:], in_=gt[h * P : (h + 1) * P, :])
@@ -142,15 +143,26 @@ def tile_list_directions_over_errors_placed_kernel(
                     g_turned[h][:, s, :], negated[:, s, :], ident[:], start=(s == 0), stop=False, is_transpose=True
                 )
 
-        def g_gather(h, on_vector, tag):
+        def g_gather_first(tag):
             picked = sb.tile([P, J], F32, name="picked", tag=tag, align_bytes=64)
-            cut = J - on_vector
-            nc.scalar.activation(picked[:, :cut], gt_sb[h][:].indirect(list_g[:, : cut // 16]), COPY)
-            if on_vector:
-                nc.vector.tensor_copy(picked[:, cut:], gt_sb[h][:].indirect(list_g[:, cut // 16 :]))
+            nc.scalar.activation(picked[:], gt_sb[0][:].indirect(list_g[:]), COPY)
             for s in range(PACK):
                 nc.tensor.matmul(
-                    g_turned[h][:, s, :], picked[:, s::PACK], ident[:], start=False, stop=(s == PACK - 1), is_transpose=True
+                    g_turned[0][:, s, :], picked[:, s::PACK], ident[:], start=False, stop=(s == PACK - 1), is_transpose=True
+                )
+
+        def g_gather_last(tag):
+            slotted = sb.tile([P, PACK, P], F32, name="slotted", tag=tag, align_bytes=64)
+            cut = ON_VECTOR
+            nc.vector.tensor_copy(
+                slotted[:, :, : cut // PACK].rearrange("p s q -> p q s"), gt_sb[1][:].indirect(list_g[:, : cut // 16])
+            )
+            picked = sb.tile([P, J - cut], F32, name="picked", tag="weight0", align_bytes=64)
+            nc.scalar.activation(picked[:], gt_sb[1][:].indirect(list_g[:, cut // 16 :]), COPY)
+            nc.scalar.copy(by_lines_out(slotted[:, :, cut // PACK :]), by_lines_in(picked[:]))
+            for s in range(PACK):
+                nc.tensor.matmul(
+                    g_turned[1][:, s, :], slotted[:, s, :], ident[:], start=False, stop=(s == PACK - 1), is_transpose=True
                 )
 
         def g_weigh(h):
@@ -219,9 +231,9 @@ def tile_list_directions_over_errors_placed_kernel(
         g_predictions(1, "x_picked2")
         x_quantize(1)
         x_threshold(3, "u_bf0")
-        g_gather(0, 0, "weight1")
+        g_gather_first("weight1")
         x_weigh(2)
-        g_gather(1, 352, "x_picked3")
+        g_gather_last("x_picked3")
         x_quantize(2)
         x_weigh(3)
         x_quantize(3)

@@ -24,11 +24,11 @@ ON_VECTOR = 352
 
 
 def by_lines_in(ap):
-    return ap.rearrange("p (b i s) -> p b s i", i=PACK, s=PACK)
+    return ap.rearrange("p (q s) -> p q s", s=PACK)
 
 
 def by_lines_out(ap):
-    return ap.rearrange("p s (b i) -> p b s i", i=PACK)
+    return ap.rearrange("p s q -> p q s")
 
 
 def tile_list_directions_over_errors_placed_kernel(

from contextlib import ExitStack

import concourse.mybir as mybir
from concourse.masks import make_identity

K, J, N, R, T, V, Q = 512, 512, 256, 256, 1024, 1024, 1024
FLOPS = 2 * J * K * N + 2 * K * R * N

F32 = mybir.dt.float32
BF16 = mybir.dt.bfloat16
I32 = mybir.dt.int32
U32 = mybir.dt.uint32
U16 = mybir.dt.uint16
U8 = mybir.dt.uint8
E4M3 = mybir.dt.float8_e4m3fn_x4
E5M2 = mybir.dt.float8_e5m2_x4
E2M1 = mybir.dt.float4_e2m1fn_x4
ALU = mybir.AluOpType
COPY = mybir.ActivationFunctionType.Copy

P = 128
PACK = 4
ON_VECTOR = 352


def by_lines_in(ap):
    return ap.rearrange("p (q s) -> p q s", s=PACK)


def by_lines_out(ap):
    return ap.rearrange("p s q -> p q s")


def tile_list_directions_over_errors_placed_kernel(
    tc, xf, ra, lo, gt, rb, pr, fkr, dr_words, dr_scales, old, offs, offs2, offs3, out
):
    nc = tc.nc
    with ExitStack() as ctx:
        sb = ctx.enter_context(tc.tile_pool(name="sb", bufs=1))
        turn = ctx.enter_context(tc.psum_pool(name="turn", bufs=6))
        sums = ctx.enter_context(tc.psum_pool(name="sums", bufs=1))

        list_x = sb.tile([P, J // 16], U16, name="list_x")
        list_g = sb.tile([P, J // 16], U16, name="list_g")
        list_out = sb.tile([P, N // 16], U16, name="list_out")
        fk4 = sb.tile([P, PACK], F32, name="fk4")
        ra4 = sb.tile([P, PACK], F32, name="ra4", tag="ra", align_bytes=64)
        rb4 = sb.tile([P, PACK], F32, name="rb4")
        lo4 = sb.tile([P, PACK], F32, name="lo4")
        gt_sb = [sb.tile([P, V], F32, name=f"gt{h}") for h in range(2)]
        pr_sb = [sb.tile([P, J], F32, name=f"pr{h}", tag=f"pr{h}", align_bytes=64) for h in range(2)]
        xf_sb = [sb.tile([P, T], F32, name=f"xf{t}") for t in range(PACK)]
        old_sb = [sb.tile([P, Q], F32, name=f"old{r}") for r in range(2)]
        page = [sb.tile([P, Q], F32, name=f"page{r}") for r in range(2)]
        dr_w = sb.tile([P, 2 * R], U8, name="dr_w", align_bytes=64)
        dr_s = sb.tile([P, R], U8, name="dr_s", align_bytes=64)
        ident = sb.tile([P, P], F32, name="ident")

        make_identity(nc, ident[:])
        nc.vector.memset(dr_s[:].bitcast(I32), 0)
        for r in range(2):
            nc.vector.memset(page[r][:], 0.0)

        nc.sync.dma_start(out=fk4[:], in_=fkr.rearrange("o (p t) -> (o p) t", t=PACK))
        nc.sync.dma_start(out=ra4[:], in_=ra.rearrange("o (p s) -> (o p) s", s=PACK))
        nc.scalar.dma_start(out=lo4[:], in_=lo.rearrange("(p t) o -> p (t o)", t=PACK))
        nc.scalar.dma_start(out=rb4[:], in_=rb.rearrange("o (p s) -> (o p) s", s=PACK))
        xf_rows = xf.rearrange("(p t) c -> t p c", t=PACK)
        nc.sync.dma_start(out=xf_sb[0][:], in_=xf_rows[0])
        nc.sync.dma_start(list_x[:], offs)
        nc.sync.dma_start(out=xf_sb[1][:], in_=xf_rows[1])
        nc.sync.dma_start(out=pr_sb[0][:], in_=pr[:P, :])
        for t in range(2, PACK):
            nc.sync.dma_start(out=xf_sb[t][:], in_=xf_rows[t])
        nc.sync.dma_start(list_g[:], offs2)
        nc.sync.dma_start(out=pr_sb[1][:], in_=pr[P:, :])
        for h in range(2):
            nc.sync.dma_start(out=gt_sb[h][:], in_=gt[h * P : (h + 1) * P, :])
        nc.sync.dma_start(out=dr_w[:].bitcast(I32), in_=dr_words[0].bitcast(I32))
        for quad in range(4):
            nc.sync.dma_start(
                out=dr_s[32 * quad : 32 * quad + 4, :].bitcast(I32),
                in_=dr_scales[0, 4 * quad : 4 * quad + 4, :].bitcast(I32),
            )
        nc.sync.dma_start(list_out[:], offs3)
        for r in range(2):
            nc.sync.dma_start(out=old_sb[r][:], in_=old[r * P : (r + 1) * P, :])

        neg_lo = sb.tile([P, PACK], F32, name="neg_lo")
        nc.scalar.activation(neg_lo[:], lo4[:], COPY, scale=-1.0)

        fk_rows = turn.tile([P, PACK, P], F32, name="turned")
        for t in range(PACK):
            nc.tensor.transpose(fk_rows[:, t, :], fk4[:, t : t + 1].to_broadcast([P, P]), ident[:])
        weight = [sb.tile([P, P, PACK], F32, name=f"weight{t}", tag=f"weight{t}", align_bytes=64) for t in range(PACK)]
        for t in range(PACK):
            nc.vector.tensor_tensor(
                weight[t][:],
                fk_rows[:, t, :].unsqueeze(2).to_broadcast([P, P, PACK]),
                ra4[:].unsqueeze(1).to_broadcast([P, P, PACK]),
                ALU.mult,
            )

        def turn_slots(src):
            turned = turn.tile([P, PACK, P], F32, name="turned")
            for s in range(PACK):
                nc.tensor.transpose(turned[:, s, :], src[:, s, :], ident[:])
            return turned

        u_turned, u_bf, u_codes, u_scales, x_picked = {}, {}, {}, {}, {}

        def x_gather(t):
            x_picked[t] = sb.tile([P, J], F32, name=f"x_picked{t}", tag=f"x_picked{t}", align_bytes=64)
            nc.scalar.activation(x_picked[t][:], xf_sb[t][:].indirect(list_x[:]), COPY)

        def x_threshold(t, tag):
            excess = sb.tile([P, PACK, P], F32, name="excess", tag=tag, align_bytes=64)
            nc.vector.tensor_scalar(
                by_lines_out(excess[:]), by_lines_in(x_picked[t][:]), neg_lo[:, t : t + 1], 0.0, ALU.add, ALU.max
            )
            u_turned[t] = turn_slots(excess)

        def x_weigh(t):
            u_bf[t] = sb.tile([P, P, PACK], BF16, name=f"u_bf{t}", tag=f"u_bf{t}", align_bytes=64)
            nc.vector.tensor_tensor(u_bf[t][:], u_turned[t][:].rearrange("p s m -> p m s"), weight[t][:], ALU.mult)

        def x_quantize(t):
            u_codes[t] = sb.tile([P, P], U32, name=f"u_codes{t}", align_bytes=64)
            u_scales[t] = sb.tile([P, P], U8, name=f"u_scales{t}", align_bytes=64)
            nc.vector.quantize_mx(u_codes[t][:].bitcast(E4M3), u_scales[t][:], u_bf[t][:].rearrange("p m s -> p (m s)"))

        g_turned, g_bf, g_codes, g_scales = {}, {}, {}, {}

        def g_predictions(h, tag):
            negated = sb.tile([P, PACK, P], F32, name="negated", tag=tag, align_bytes=64)
            if h == 0:
                nc.vector.tensor_scalar(by_lines_out(negated[:]), by_lines_in(pr_sb[h][:]), -1.0, None, ALU.mult)
            else:
                nc.scalar.activation(by_lines_out(negated[:]), by_lines_in(pr_sb[h][:]), COPY, scale=-1.0)
            g_turned[h] = turn.tile([P, PACK, P], F32, name="turned")
            for s in range(PACK):
                nc.tensor.matmul(
                    g_turned[h][:, s, :], negated[:, s, :], ident[:], start=(s == 0), stop=False, is_transpose=True
                )

        def g_gather_first(tag):
            picked = sb.tile([P, J], F32, name="picked", tag=tag, align_bytes=64)
            nc.scalar.activation(picked[:], gt_sb[0][:].indirect(list_g[:]), COPY)
            for s in range(PACK):
                nc.tensor.matmul(
                    g_turned[0][:, s, :], picked[:, s::PACK], ident[:], start=False, stop=(s == PACK - 1), is_transpose=True
                )

        def g_gather_last(tag):
            slotted = sb.tile([P, PACK, P], F32, name="slotted", tag=tag, align_bytes=64)
            cut = ON_VECTOR
            nc.vector.tensor_copy(
                slotted[:, :, : cut // PACK].rearrange("p s q -> p q s"), gt_sb[1][:].indirect(list_g[:, : cut // 16])
            )
            picked = sb.tile([P, J - cut], F32, name="picked", tag="weight0", align_bytes=64)
            nc.scalar.activation(picked[:], gt_sb[1][:].indirect(list_g[:, cut // 16 :]), COPY)
            nc.scalar.copy(by_lines_out(slotted[:, :, cut // PACK :]), by_lines_in(picked[:]))
            for s in range(PACK):
                nc.tensor.matmul(
                    g_turned[1][:, s, :], slotted[:, s, :], ident[:], start=False, stop=(s == PACK - 1), is_transpose=True
                )

        def g_weigh(h):
            g_bf[h] = sb.tile([P, P, PACK], BF16, name=f"g_bf{h}", align_bytes=64)
            nc.vector.tensor_tensor(
                g_bf[h][:], g_turned[h][:].rearrange("p s n -> p n s"), rb4[:].unsqueeze(1).to_broadcast([P, P, PACK]), ALU.mult
            )

        w_sum, w_bf, w_codes, w_scales = {}, {}, {}, {}

        def first_product(h):
            g_codes[h] = sb.tile([P, P], U32, name=f"g_codes{h}", align_bytes=64)
            g_scales[h] = sb.tile([P, P], U8, name=f"g_scales{h}", align_bytes=64)
            nc.vector.quantize_mx(g_codes[h][:].bitcast(E5M2), g_scales[h][:], g_bf[h][:].rearrange("p n s -> p (n s)"))
            w_sum[h] = sums.tile([P, PACK, P], F32, name=f"w_sum{h}")
            for t in range(PACK):
                nc.tensor.matmul_mx(
                    out=w_sum[h][:, t, :],
                    lhsT=u_codes[t][:].bitcast(E4M3),
                    lhsT_scale=u_scales[t][:],
                    rhs=g_codes[h][:].bitcast(E5M2),
                    rhs_scale=g_scales[h][:],
                    start=True,
                    stop=True,
                )
            w_bf[h] = sb.tile([P, P, PACK], BF16, name=f"w_bf{h}", align_bytes=64)
            nc.scalar.copy(w_bf[h][:], w_sum[h][:].rearrange("p t n -> p n t"))

        v_sum = {}

        def second_product(h):
            w_codes[h] = sb.tile([P, P], U32, name=f"w_codes{h}", align_bytes=64)
            w_scales[h] = sb.tile([P, P], U8, name=f"w_scales{h}", align_bytes=64)
            nc.vector.quantize_mx(w_codes[h][:].bitcast(E5M2), w_scales[h][:], w_bf[h][:].rearrange("p n t -> p (n t)"))
            for r in range(2):
                v_sum[r, h] = turn.tile([P, P], F32, name="turned")
                nc.tensor.matmul_mx(
                    out=v_sum[r, h][:],
                    lhsT=dr_w[:, 2 * P * r : 2 * P * (r + 1)].bitcast(E2M1),
                    lhsT_scale=dr_s[:, P * r : P * (r + 1)],
                    rhs=w_codes[h][:].bitcast(E5M2),
                    rhs_scale=w_scales[h][:],
                    start=True,
                    stop=True,
                )

        def place(h):
            places = list_out[:, h * P // 16 : (h + 1) * P // 16]
            v_sb = [sb.tile([P, P], F32, name=f"v_sb{r}{h}") for r in range(2)]
            nc.vector.tensor_copy(v_sb[0][:], v_sum[0, h][:])
            nc.scalar.copy(v_sb[1][:], v_sum[1, h][:])
            nc.vector.tensor_copy(page[0][:].indirect(places), v_sb[0][:])
            nc.scalar.activation(page[1][:].indirect(places), v_sb[1][:], COPY)

        x_gather(0)
        x_gather(1)
        x_threshold(0, "ra")
        g_predictions(0, "x_picked0")
        x_gather(2)
        x_threshold(1, "pr0")
        x_weigh(0)
        x_gather(3)
        x_threshold(2, "weight0")
        x_weigh(1)
        x_quantize(0)
        g_predictions(1, "x_picked2")
        x_quantize(1)
        x_threshold(3, "u_bf0")
        g_gather_first("weight1")
        x_weigh(2)
        g_gather_last("x_picked3")
        x_quantize(2)
        x_weigh(3)
        x_quantize(3)
        g_weigh(0)
        g_weigh(1)
        first_product(0)
        first_product(1)
        second_product(0)
        second_product(1)
        place(0)
        place(1)
        for r in range(2):
            for c in range(2):
                cols = slice(c * Q // 2, (c + 1) * Q // 2)
                result = sb.tile([P, Q // 2], F32, name=f"result{r}{c}")
                nc.vector.scalar_tensor_tensor(
                    result[:], page[r][:, cols], 0.05, old_sb[r][:, cols], ALU.mult, ALU.add
                )
                queue = nc.sync if c == 0 else nc.scalar
                queue.dma_start(out=out[r * P : (r + 1) * P, cols], in_=result[:])
